import numpy as np
import ml_dtypes


def mxq(x, axis, fmt="e4m3"):
    dtype, down = {"e4m3": (ml_dtypes.float8_e4m3fn, 7), "e5m2": (ml_dtypes.float8_e5m2, 14)}[fmt]
    v = np.moveaxis(np.asarray(x, np.float32).astype(ml_dtypes.bfloat16).astype(np.float64), axis, -1)
    blocks = v.reshape(v.shape[:-1] + (-1, 32))
    amax = np.abs(blocks).max(-1, keepdims=True)
    byte = np.maximum(np.where(amax > 0, np.frexp(amax)[1] - 1 + 127, 0) - down, 1)
    scale = np.exp2(byte - 127.0)
    codes = (blocks / scale).astype(np.float32).astype(dtype).astype(np.float64)
    return np.moveaxis((codes * scale).reshape(v.shape), -1, axis)


WIDE = False


def mx_kscale(k):
    if not WIDE:
        return np.ones(k)
    levels = np.array([10, -10, 5, -5, 0])
    if k % 512:
        return np.exp2(np.random.permutation(np.resize(levels, k // 32))).repeat(32)
    a = np.empty((k // 512, 16))
    for p in range(k // 512):
        a[p, :8] = np.random.permutation(np.resize(levels, 8))
        for g in range(8):
            far = levels[np.abs(levels - a[p, g]) >= 10]
            a[p, g + 8] = far[np.random.randint(len(far))]
    return np.exp2(a.ravel()).repeat(32)


def f64(x):
    return np.asarray(x).astype(np.float64)


def striped(idx):
    return np.tile(idx.reshape(-1, 16).T, (8, 1)).astype(np.uint16)


def unstriped(offs):
    return offs[:16].T.reshape(-1).astype(np.int64)


def silu(v):
    return v / (1.0 + np.exp(-np.maximum(v, -700.0)))


K, T, D, S, V, H, N = 512, 2048, 3, 512, 256, 512, 512
P = 2 ** 7


def setup_inputs():
    n = np.random.standard_normal
    s = mx_kscale(K)[:, None]
    u = mx_kscale(H)
    q = np.random.permutation(S)
    return {
        "xT": (n((K, T)) * s).astype(np.float32),
        "w1": (n((K, H)) / np.sqrt(K) / s * u).astype(np.float32),
        "w2": (n((H, N)) / np.sqrt(H) / u[:, None]).astype(np.float32),
        "gate": np.tile(np.random.uniform(0.2, 1.0, (D, 1, V)) / np.sqrt(D), (1, P, 1)).astype(np.float32),
        "offs": striped(np.random.permutation(T)[:S]),
        "pos1": striped(q[:V]),
        "pos2": striped(q[V:]),
        "pos3": striped(np.random.permutation(S)[:V]),
    }


def reference(xT, w1, w2, gate, offs, pos1, pos2, pos3):
    h = silu(mxq(f64(w1), 0, "e4m3").T @ mxq(f64(xT)[:, unstriped(offs)], 0, "e4m3"))
    z = sum(f64(gate)[d, :1] * h[:, unstriped(p)] for d, p in enumerate((pos1, pos2, pos3)))
    return mxq(f64(w2), 0, "e4m3").T @ mxq(z, 0, "e4m3")

@@ -1,0 +1,153 @@
+from contextlib import ExitStack
+
+import concourse.mybir as mybir
+
+FLOPS = 2 * 512 * 512 * 512 + 2 * 512 * 512 * 256
+
+F32 = mybir.dt.float32
+BF16 = mybir.dt.bfloat16
+U32 = mybir.dt.uint32
+U16 = mybir.dt.uint16
+U8 = mybir.dt.uint8
+FP8X4 = mybir.dt.float8_e4m3fn_x4
+MULT = mybir.AluOpType.mult
+ADD = mybir.AluOpType.add
+SILU = mybir.ActivationFunctionType.Silu
+
+P = 128
+K, T, S, V, H, N, D = 512, 2048, 512, 256, 512, 512, 3
+PACK = 4
+
+
+def tile_picked_sage_silu_e_kernel(tc, xT, w1, w2, gate, offs, pos1, pos2, pos3, out):
+    nc = tc.nc
+    with ExitStack() as ctx:
+        keep = ctx.enter_context(tc.tile_pool(name="keep", bufs=1))
+        psum = ctx.enter_context(tc.psum_pool(name="psum", bufs=1))
+
+        warm = keep.tile([P, 1], F32, name="warm")
+        warm_out = keep.tile([P, 1], F32, name="warm_out")
+        nc.vector.memset(warm[:], 0.0)
+        nc.scalar.activation(warm_out[:], warm[:], SILU)
+
+        offs_t = keep.tile([P, S // 16], U16, name="offs_t")
+        nc.sync.dma_start(offs_t[:], offs)
+        planes = [keep.tile([P, T], F32, name=f"plane{j}") for j in range(PACK)]
+        x_view = xT.rearrange("(p j) t -> p j t", j=PACK)
+        w1_raw = keep.tile([P, PACK, H], F32, name="w1_raw")
+        w2_raw = keep.tile([P, PACK, N], F32, name="w2_raw")
+        gates = keep.tile([P, D, V], F32, name="gates")
+        pos_t = [keep.tile([P, V // 16], U16, name=f"pos_t{d}") for d in range(D)]
+
+        nc.sync.dma_start(planes[0][:], x_view[:, 0, :])
+        nc.sync.dma_start(planes[1][:], x_view[:, 1, :])
+        nc.sync.dma_start(w1_raw[:], w1.rearrange("(p j) c -> p j c", j=PACK))
+        nc.sync.dma_start(planes[2][:], x_view[:, 2, :])
+        nc.sync.dma_start(planes[3][:], x_view[:, 3, :])
+        for d, pos in enumerate((pos1, pos2, pos3)):
+            nc.sync.dma_start(pos_t[d][:], pos)
+        nc.sync.dma_start(gates[:], gate.rearrange("d p v -> p d v"))
+        nc.sync.dma_start(w2_raw[:], w2.rearrange("(p j) m -> p j m", j=PACK))
+
+        xg = keep.tile([P, S, PACK], BF16, align_bytes=64, name="xg")
+        x_codes = keep.tile([P, S], U32, align_bytes=64, name="x_codes")
+        x_scales = keep.tile([P, S], U8, align_bytes=64, name="x_scales")
+        w1g = keep.tile([P, PACK * H], BF16, align_bytes=64, name="w1g")
+        w1_codes = keep.tile([P, H], U32, align_bytes=64, name="w1_codes")
+        w1_scales = keep.tile([P, H], U8, align_bytes=64, name="w1_scales")
+        w2g = keep.tile([P, N, PACK], BF16, align_bytes=64, name="w2g")
+        w2_codes = keep.tile([P, N], U32, align_bytes=64, name="w2_codes")
+        w2_scales = keep.tile([P, N], U8, align_bytes=64, name="w2_scales")
+
+        def quantize(codes, scales, grouped, a, b):
+            nc.vector.quantize_mx(out=codes[:, a:b].bitcast(FP8X4), scales=scales[:, a:b], in_=grouped[:, PACK * a : PACK * b])
+
+        xg_flat = xg[:].rearrange("p s j -> p (s j)")
+        w2g_flat = w2g[:].rearrange("p m j -> p (m j)")
+
+        nc.vector.tensor_copy(xg[:, :, 0], planes[0][:].indirect(offs_t[:]))
+        nc.vector.tensor_copy(xg[:, :, 1], planes[1][:].indirect(offs_t[:]))
+
+        w1_out = w1g[:].rearrange("p (t m j) -> p m t j", t=4, j=PACK)
+        w1_in = w1_raw[:].rearrange("p j (m t) -> p m t j", t=4)
+        for u in range(2):
+            nc.scalar.copy(w1_out[:, :, 2 * u : 2 * u + 2, :], w1_in[:, :, 2 * u : 2 * u + 2, :])
+        nc.vector.tensor_copy(xg[:, :, 2], planes[2][:].indirect(offs_t[:]))
+        for u in range(2):
+            quantize(w1_codes, w1_scales, w1g[:], 256 * u, 256 * u + 256)
+        for u in range(2):
+            nc.vector.tensor_copy(xg[:, 256 * u : 256 * u + 256, 3], planes[3][:].indirect(offs_t[:, 16 * u : 16 * u + 16]))
+        for u in range(2):
+            quantize(x_codes, x_scales, xg_flat, 256 * u, 256 * u + 256)
+
+        banks = [psum.tile([P, S], F32, name=f"bank{t}") for t in range(4)]
+        for u in range(2):
+            cols = slice(256 * u, 256 * u + 256)
+            for t in range(4):
+                nc.tensor.matmul_mx(
+                    out=banks[t][:, cols],
+                    lhsT=w1_codes[:, 128 * t : 128 * t + 128].bitcast(FP8X4),
+                    lhsT_scale=w1_scales[:, 128 * t : 128 * t + 128],
+                    rhs=x_codes[:, cols].bitcast(FP8X4),
+                    rhs_scale=x_scales[:, cols],
+                    start=True,
+                    stop=True,
+                )
+
+        h = [keep.tile([P, S], F32, name=f"h{t}") for t in range(4)]
+        for u in range(2):
+            nc.scalar.activation(h[0][:, 256 * u : 256 * u + 256], banks[0][:, 256 * u : 256 * u + 256], SILU)
+        for t in range(1, 4):
+            nc.scalar.activation(h[t][:], banks[t][:], SILU)
+
+        w2_in4 = w2_raw[:].rearrange("p j (c i) -> p c j i", i=4)
+        w2_out4 = w2g[:].rearrange("p (c i) j -> p c j i", i=4)
+        for u in range(2):
+            nc.scalar.copy(w2_out4[:, 64 * u : 64 * u + 64], w2_in4[:, 64 * u : 64 * u + 64])
+
+        terms = [keep.tile([P, 4, V], F32, name=f"term{d}") for d in range(D)]
+        part = keep.tile([P, 4, V], F32, name="part")
+        for t in range(4):
+            for d in range(D):
+                nc.vector.tensor_tensor(terms[d][:, t, :], h[t][:].indirect(pos_t[d][:]), gates[:, d, :], MULT)
+            if t == 2:
+                for u in range(2):
+                    quantize(w2_codes, w2_scales, w2g_flat, 256 * u, 256 * u + 256)
+            nc.vector.tensor_tensor(part[:, t, :], terms[0][:, t, :], terms[1][:, t, :], ADD)
+
+        zg = keep.tile([P, V, PACK], BF16, align_bytes=64, name="zg")
+        zg_flat = zg[:].rearrange("p v j -> p (v j)")
+        z_codes = keep.tile([P, V], U32, align_bytes=64, name="z_codes")
+        z_scales = keep.tile([P, V], U8, align_bytes=64, name="z_scales")
+        z_out = zg[:].rearrange("p (c i) t -> p c t i", i=4)
+        part_in = part[:].rearrange("p t (c i) -> p c t i", i=4)
+        last_in = terms[2][:].rearrange("p t (c i) -> p c t i", i=4)
+        for u in range(2):
+            c = slice(32 * u, 32 * u + 32)
+            nc.vector.tensor_tensor(z_out[:, c], part_in[:, c], last_in[:, c], ADD)
+        for u in range(2):
+            quantize(z_codes, z_scales, zg_flat, 128 * u, 128 * u + 128)
+
+        o_banks = [psum.tile([P, 2, 128], F32, name=f"o_bank{b}") for b in range(4)]
+        staged = [keep.tile([P, 2, 128], F32, name=f"staged{b}") for b in range(4)]
+        out_view = out.rearrange("(m p) v -> p m v", p=P)
+        for u in range(2):
+            for g in range(2):
+                b = 2 * u + g
+                for i in range(2):
+                    m = 2 * g + i
+                    nc.tensor.matmul_mx(
+                        out=o_banks[b][:, i, :],
+                        lhsT=w2_codes[:, 128 * m : 128 * m + 128].bitcast(FP8X4),
+                        lhsT_scale=w2_scales[:, 128 * m : 128 * m + 128],
+                        rhs=z_codes[:, 128 * u : 128 * u + 128].bitcast(FP8X4),
+                        rhs_scale=z_scales[:, 128 * u : 128 * u + 128],
+                        start=True,
+                        stop=True,
+                    )
+                if g == 0:
+                    nc.scalar.copy(staged[b][:], o_banks[b][:])
+                    nc.sync.dma_start(out_view[:, 2 * g : 2 * g + 2, 128 * u : 128 * u + 128], staged[b][:])
+                else:
+                    nc.vector.tensor_copy(staged[b][:], o_banks[b][:])
+                    nc.scalar.dma_start(out_view[:, 2 * g : 2 * g + 2, 128 * u : 128 * u + 128], staged[b][:])

@@ -1,6 +1,7 @@
 from contextlib import ExitStack
 
 import concourse.mybir as mybir
+from concourse.masks import make_identity
 
 FLOPS = 2 * 512 * 512 * 512 + 2 * 512 * 512 * 256
 
@@ -25,11 +26,6 @@ def tile_picked_sage_silu_e_kernel(tc, xT, w1, w2, gate, offs, pos1, pos2, pos3,
         keep = ctx.enter_context(tc.tile_pool(name="keep", bufs=1))
         psum = ctx.enter_context(tc.psum_pool(name="psum", bufs=1))
 
-        warm = keep.tile([P, 1], F32, name="warm")
-        warm_out = keep.tile([P, 1], F32, name="warm_out")
-        nc.vector.memset(warm[:], 0.0)
-        nc.scalar.activation(warm_out[:], warm[:], SILU)
-
         offs_t = keep.tile([P, S // 16], U16, name="offs_t")
         nc.sync.dma_start(offs_t[:], offs)
         planes = [keep.tile([P, T], F32, name=f"plane{j}") for j in range(PACK)]
@@ -39,22 +35,29 @@ def tile_picked_sage_silu_e_kernel(tc, xT, w1, w2, gate, offs, pos1, pos2, pos3,
         gates = keep.tile([P, D, V], F32, name="gates")
         pos_t = [keep.tile([P, V // 16], U16, name=f"pos_t{d}") for d in range(D)]
 
-        nc.sync.dma_start(planes[0][:], x_view[:, 0, :])
-        nc.sync.dma_start(planes[1][:], x_view[:, 1, :])
+        for j in range(PACK):
+            nc.sync.dma_start(planes[j][:], x_view[:, j, :])
         nc.sync.dma_start(w1_raw[:], w1.rearrange("(p j) c -> p j c", j=PACK))
-        nc.sync.dma_start(planes[2][:], x_view[:, 2, :])
-        nc.sync.dma_start(planes[3][:], x_view[:, 3, :])
         for d, pos in enumerate((pos1, pos2, pos3)):
             nc.sync.dma_start(pos_t[d][:], pos)
         nc.sync.dma_start(gates[:], gate.rearrange("d p v -> p d v"))
-        nc.sync.dma_start(w2_raw[:], w2.rearrange("(p j) m -> p j m", j=PACK))
+        w2_view = w2.rearrange("(g j r) m -> j g r m", j=PACK, r=8)
+        for j in range(PACK):
+            nc.sync.dma_start(w2_raw[:, j, :], w2_view[j])
+
+        warm = keep.tile([P, 1], F32, name="warm")
+        warm_out = keep.tile([P, 1], F32, name="warm_out")
+        nc.vector.memset(warm[:], 0.0)
+        nc.scalar.activation(warm_out[:], warm[:], SILU)
+        ident = keep.tile([P, P], F32, name="ident")
+        make_identity(nc, ident[:])
 
         xg = keep.tile([P, S, PACK], BF16, align_bytes=64, name="xg")
         x_codes = keep.tile([P, S], U32, align_bytes=64, name="x_codes")
         x_scales = keep.tile([P, S], U8, align_bytes=64, name="x_scales")
-        w1g = keep.tile([P, PACK * H], BF16, align_bytes=64, name="w1g")
-        w1_codes = keep.tile([P, H], U32, align_bytes=64, name="w1_codes")
-        w1_scales = keep.tile([P, H], U8, align_bytes=64, name="w1_scales")
+        w1g = [keep.tile([P, P, PACK], BF16, align_bytes=64, name=f"w1g{t}") for t in range(4)]
+        w1_codes = [keep.tile([P, P], U32, align_bytes=64, name=f"w1_codes{t}") for t in range(4)]
+        w1_scales = [keep.tile([P, P], U8, align_bytes=64, name=f"w1_scales{t}") for t in range(4)]
         w2g = keep.tile([P, N, PACK], BF16, align_bytes=64, name="w2g")
         w2_codes = keep.tile([P, N], U32, align_bytes=64, name="w2_codes")
         w2_scales = keep.tile([P, N], U8, align_bytes=64, name="w2_scales")
@@ -65,79 +68,113 @@ def tile_picked_sage_silu_e_kernel(tc, xT, w1, w2, gate, offs, pos1, pos2, pos3,
         xg_flat = xg[:].rearrange("p s j -> p (s j)")
         w2g_flat = w2g[:].rearrange("p m j -> p (m j)")
 
-        nc.vector.tensor_copy(xg[:, :, 0], planes[0][:].indirect(offs_t[:]))
-        nc.vector.tensor_copy(xg[:, :, 1], planes[1][:].indirect(offs_t[:]))
-
-        w1_out = w1g[:].rearrange("p (t m j) -> p m t j", t=4, j=PACK)
-        w1_in = w1_raw[:].rearrange("p j (m t) -> p m t j", t=4)
-        for u in range(2):
-            nc.scalar.copy(w1_out[:, :, 2 * u : 2 * u + 2, :], w1_in[:, :, 2 * u : 2 * u + 2, :])
-        nc.vector.tensor_copy(xg[:, :, 2], planes[2][:].indirect(offs_t[:]))
-        for u in range(2):
-            quantize(w1_codes, w1_scales, w1g[:], 256 * u, 256 * u + 256)
+        for j in range(3):
+            nc.vector.tensor_copy(xg[:, :, j], planes[j][:].indirect(offs_t[:]))
         for u in range(2):
             nc.vector.tensor_copy(xg[:, 256 * u : 256 * u + 256, 3], planes[3][:].indirect(offs_t[:, 16 * u : 16 * u + 16]))
         for u in range(2):
             quantize(x_codes, x_scales, xg_flat, 256 * u, 256 * u + 256)
 
+        w1_in = w1_raw[:].rearrange("p j (g t r) -> t p g r j", t=4, r=8)
         banks = [psum.tile([P, S], F32, name=f"bank{t}") for t in range(4)]
-        for u in range(2):
-            cols = slice(256 * u, 256 * u + 256)
-            for t in range(4):
-                nc.tensor.matmul_mx(
-                    out=banks[t][:, cols],
-                    lhsT=w1_codes[:, 128 * t : 128 * t + 128].bitcast(FP8X4),
-                    lhsT_scale=w1_scales[:, 128 * t : 128 * t + 128],
-                    rhs=x_codes[:, cols].bitcast(FP8X4),
-                    rhs_scale=x_scales[:, cols],
-                    start=True,
-                    stop=True,
-                )
-
         h = [keep.tile([P, S], F32, name=f"h{t}") for t in range(4)]
+
+        def cast_w1(t, copy):
+            copy(w1g[t][:].rearrange("p (g r) j -> p g r j", r=8), w1_in[t])
+
+        def layer1(t):
+            quantize(w1_codes[t], w1_scales[t], w1g[t][:].rearrange("p m j -> p (m j)"), 0, P)
+            nc.tensor.matmul_mx(
+                out=banks[t][:],
+                lhsT=w1_codes[t][:].bitcast(FP8X4),
+                lhsT_scale=w1_scales[t][:],
+                rhs=x_codes[:].bitcast(FP8X4),
+                rhs_scale=x_scales[:],
+                start=True,
+                stop=True,
+            )
+
+        cast_w1(0, nc.vector.tensor_copy)
+        cast_w1(1, nc.scalar.copy)
+        cast_w1(2, nc.scalar.copy)
+        layer1(0)
         for u in range(2):
             nc.scalar.activation(h[0][:, 256 * u : 256 * u + 256], banks[0][:, 256 * u : 256 * u + 256], SILU)
-        for t in range(1, 4):
-            nc.scalar.activation(h[t][:], banks[t][:], SILU)
+        layer1(1)
+        nc.scalar.activation(h[1][:], banks[1][:], SILU)
+        layer1(2)
+        cast_w1(3, nc.scalar.copy)
+        nc.scalar.activation(h[2][:], banks[2][:], SILU)
+
+        terms = [keep.tile([P, 4, V], F32, name=f"term{d}") for d in range(D)]
+        parts = [psum.tile([P, 4, 128], F32, name=f"part{u}") for u in range(2)]
+
+        def fetch(t, d):
+            nc.vector.tensor_tensor(terms[d][:, t, :], h[t][:].indirect(pos_t[d][:]), gates[:, d, :], MULT)
+
+        def add_two(t):
+            flipped = psum.tile([P, 2, 128], F32, name=f"flipped{t % 2}")
+            for u in range(2):
+                for d in range(2):
+                    nc.tensor.matmul(flipped[:, u, :], terms[d][:, t, 128 * u : 128 * u + 128], ident[:], is_transpose=True, start=d == 0, stop=d == 1)
+            flat = keep.tile([P, 2, 128], F32, name=f"flat{t}")
+            nc.scalar.copy(flat[:], flipped[:])
+            for u in range(2):
+                nc.tensor.transpose(parts[u][:, t, :], flat[:, u, :], ident[:])
 
         w2_in4 = w2_raw[:].rearrange("p j (c i) -> p c j i", i=4)
         w2_out4 = w2g[:].rearrange("p (c i) j -> p c j i", i=4)
-        for u in range(2):
-            nc.scalar.copy(w2_out4[:, 64 * u : 64 * u + 64], w2_in4[:, 64 * u : 64 * u + 64])
 
-        terms = [keep.tile([P, 4, V], F32, name=f"term{d}") for d in range(D)]
-        part = keep.tile([P, 4, V], F32, name="part")
-        for t in range(4):
-            for d in range(D):
-                nc.vector.tensor_tensor(terms[d][:, t, :], h[t][:].indirect(pos_t[d][:]), gates[:, d, :], MULT)
-            if t == 2:
-                for u in range(2):
-                    quantize(w2_codes, w2_scales, w2g_flat, 256 * u, 256 * u + 256)
-            nc.vector.tensor_tensor(part[:, t, :], terms[0][:, t, :], terms[1][:, t, :], ADD)
+        def cast_w2(q):
+            nc.scalar.copy(w2_out4[:, 32 * q : 32 * q + 32], w2_in4[:, 32 * q : 32 * q + 32])
+
+        fetch(0, 0)
+        fetch(0, 1)
+        add_two(0)
+        layer1(3)
+        nc.scalar.activation(h[3][:], banks[3][:], SILU)
+        fetch(0, 2)
+        fetch(1, 0)
+        fetch(1, 1)
+        add_two(1)
+        cast_w2(0)
+        fetch(1, 2)
+        cast_w2(1)
+        fetch(2, 0)
+        fetch(2, 1)
+        add_two(2)
+        cast_w2(2)
+        quantize(w2_codes, w2_scales, w2g_flat, 0, 256)
+        fetch(3, 0)
+        fetch(3, 1)
+        add_two(3)
+        cast_w2(3)
+        fetch(2, 2)
+        quantize(w2_codes, w2_scales, w2g_flat, 256, 512)
+        fetch(3, 2)
 
         zg = keep.tile([P, V, PACK], BF16, align_bytes=64, name="zg")
         zg_flat = zg[:].rearrange("p v j -> p (v j)")
         z_codes = keep.tile([P, V], U32, align_bytes=64, name="z_codes")
         z_scales = keep.tile([P, V], U8, align_bytes=64, name="z_scales")
         z_out = zg[:].rearrange("p (c i) t -> p c t i", i=4)
-        part_in = part[:].rearrange("p t (c i) -> p c t i", i=4)
         last_in = terms[2][:].rearrange("p t (c i) -> p c t i", i=4)
         for u in range(2):
             c = slice(32 * u, 32 * u + 32)
-            nc.vector.tensor_tensor(z_out[:, c], part_in[:, c], last_in[:, c], ADD)
+            nc.vector.tensor_tensor(z_out[:, c], parts[u][:].rearrange("p t (c i) -> p c t i", i=4), last_in[:, c], ADD)
         for u in range(2):
             quantize(z_codes, z_scales, zg_flat, 128 * u, 128 * u + 128)
 
-        o_banks = [psum.tile([P, 2, 128], F32, name=f"o_bank{b}") for b in range(4)]
         staged = [keep.tile([P, 2, 128], F32, name=f"staged{b}") for b in range(4)]
         out_view = out.rearrange("(m p) v -> p m v", p=P)
         for u in range(2):
             for g in range(2):
                 b = 2 * u + g
+                o_bank = psum.tile([P, 2, 128], F32, name=f"bank{b}")
                 for i in range(2):
                     m = 2 * g + i
                     nc.tensor.matmul_mx(
-                        out=o_banks[b][:, i, :],
+                        out=o_bank[:, i, :],
                         lhsT=w2_codes[:, 128 * m : 128 * m + 128].bitcast(FP8X4),
                         lhsT_scale=w2_scales[:, 128 * m : 128 * m + 128],
                         rhs=z_codes[:, 128 * u : 128 * u + 128].bitcast(FP8X4),
@@ -146,8 +183,8 @@ def tile_picked_sage_silu_e_kernel(tc, xT, w1, w2, gate, offs, pos1, pos2, pos3,
                         stop=True,
                     )
                 if g == 0:
-                    nc.scalar.copy(staged[b][:], o_banks[b][:])
+                    nc.scalar.copy(staged[b][:], o_bank[:])
                     nc.sync.dma_start(out_view[:, 2 * g : 2 * g + 2, 128 * u : 128 * u + 128], staged[b][:])
                 else:
-                    nc.vector.tensor_copy(staged[b][:], o_banks[b][:])
+                    nc.vector.tensor_copy(staged[b][:], o_bank[:])
                     nc.scalar.dma_start(out_view[:, 2 * g : 2 * g + 2, 128 * u : 128 * u + 128], staged[b][:])

@@ -39,8 +39,8 @@ def tile_picked_sage_silu_e_kernel(tc, xT, w1, w2, gate, offs, pos1, pos2, pos3,
             nc.sync.dma_start(planes[j][:], x_view[:, j, :])
         nc.sync.dma_start(w1_raw[:], w1.rearrange("(p j) c -> p j c", j=PACK))
         for d, pos in enumerate((pos1, pos2, pos3)):
+            nc.sync.dma_start(gates[:, d, :], gate[d])
             nc.sync.dma_start(pos_t[d][:], pos)
-        nc.sync.dma_start(gates[:], gate.rearrange("d p v -> p d v"))
         w2_view = w2.rearrange("(g j r) m -> j g r m", j=PACK, r=8)
         for j in range(PACK):
             nc.sync.dma_start(w2_raw[:, j, :], w2_view[j])
@@ -80,31 +80,39 @@ def tile_picked_sage_silu_e_kernel(tc, xT, w1, w2, gate, offs, pos1, pos2, pos3,
         h = [keep.tile([P, S], F32, name=f"h{t}") for t in range(4)]
 
         def cast_w1(t, copy):
-            copy(w1g[t][:].rearrange("p (g r) j -> p g r j", r=8), w1_in[t])
+            grouped = w1g[t][:].rearrange("p (g r) j -> p g r j", r=8)
+            copy(grouped, w1_in[t])
 
-        def layer1(t):
+        def quantize_w1(t):
             quantize(w1_codes[t], w1_scales[t], w1g[t][:].rearrange("p m j -> p (m j)"), 0, P)
+
+        def layer1(bank, t, cols):
             nc.tensor.matmul_mx(
-                out=banks[t][:],
+                out=bank,
                 lhsT=w1_codes[t][:].bitcast(FP8X4),
                 lhsT_scale=w1_scales[t][:],
-                rhs=x_codes[:].bitcast(FP8X4),
-                rhs_scale=x_scales[:],
+                rhs=x_codes[:, cols].bitcast(FP8X4),
+                rhs_scale=x_scales[:, cols],
                 start=True,
                 stop=True,
             )
 
         cast_w1(0, nc.vector.tensor_copy)
         cast_w1(1, nc.scalar.copy)
-        cast_w1(2, nc.scalar.copy)
-        layer1(0)
-        for u in range(2):
-            nc.scalar.activation(h[0][:, 256 * u : 256 * u + 256], banks[0][:, 256 * u : 256 * u + 256], SILU)
-        layer1(1)
-        nc.scalar.activation(h[1][:], banks[1][:], SILU)
-        layer1(2)
-        cast_w1(3, nc.scalar.copy)
-        nc.scalar.activation(h[2][:], banks[2][:], SILU)
+        quantize_w1(0)
+        cast_w1(2, nc.vector.tensor_copy)
+        quantize_w1(1)
+        cast_w1(3, nc.vector.tensor_copy)
+        quantize_w1(2)
+        quantize_w1(3)
+        bank0b = psum.tile([P, 256], F32, name="part0")
+        for u, bank in enumerate((banks[0][:, 0:256], bank0b[:])):
+            cols = slice(256 * u, 256 * u + 256)
+            layer1(bank, 0, cols)
+            nc.scalar.activation(h[0][:, cols], bank, SILU)
+        for t in range(1, 4):
+            layer1(banks[t][:], t, slice(0, S))
+            nc.scalar.activation(h[t][:], banks[t][:], SILU)
 
         terms = [keep.tile([P, 4, V], F32, name=f"term{d}") for d in range(D)]
         parts = [psum.tile([P, 4, 128], F32, name=f"part{u}") for u in range(2)]
@@ -125,45 +133,26 @@ def tile_picked_sage_silu_e_kernel(tc, xT, w1, w2, gate, offs, pos1, pos2, pos3,
         w2_in4 = w2_raw[:].rearrange("p j (c i) -> p c j i", i=4)
         w2_out4 = w2g[:].rearrange("p (c i) j -> p c j i", i=4)
 
-        def cast_w2(q):
-            nc.scalar.copy(w2_out4[:, 32 * q : 32 * q + 32], w2_in4[:, 32 * q : 32 * q + 32])
+        for t in range(4):
+            fetch(t, 0)
+            fetch(t, 1)
+            add_two(t)
+            nc.scalar.copy(w2_out4[:, 32 * t : 32 * t + 32], w2_in4[:, 32 * t : 32 * t + 32])
+        for t in range(4):
+            fetch(t, 2)
+            if t < 2:
+                quantize(w2_codes, w2_scales, w2g_flat, 256 * t, 256 * t + 256)
 
-        fetch(0, 0)
-        fetch(0, 1)
-        add_two(0)
-        layer1(3)
-        nc.scalar.activation(h[3][:], banks[3][:], SILU)
-        fetch(0, 2)
-        fetch(1, 0)
-        fetch(1, 1)
-        add_two(1)
-        cast_w2(0)
-        fetch(1, 2)
-        cast_w2(1)
-        fetch(2, 0)
-        fetch(2, 1)
-        add_two(2)
-        cast_w2(2)
-        quantize(w2_codes, w2_scales, w2g_flat, 0, 256)
-        fetch(3, 0)
-        fetch(3, 1)
-        add_two(3)
-        cast_w2(3)
-        fetch(2, 2)
-        quantize(w2_codes, w2_scales, w2g_flat, 256, 512)
-        fetch(3, 2)
-
-        zg = keep.tile([P, V, PACK], BF16, align_bytes=64, name="zg")
-        zg_flat = zg[:].rearrange("p v j -> p (v j)")
-        z_codes = keep.tile([P, V], U32, align_bytes=64, name="z_codes")
-        z_scales = keep.tile([P, V], U8, align_bytes=64, name="z_scales")
-        z_out = zg[:].rearrange("p (c i) t -> p c t i", i=4)
-        last_in = terms[2][:].rearrange("p t (c i) -> p c t i", i=4)
+        zg = [keep.tile([P, 128, PACK], BF16, align_bytes=64, name=f"zg{u}") for u in range(2)]
+        z_codes = [keep.tile([P, 128], U32, align_bytes=64, name=f"z_codes{u}") for u in range(2)]
+        z_scales = [keep.tile([P, 128], U8, align_bytes=64, name=f"z_scales{u}") for u in range(2)]
         for u in range(2):
-            c = slice(32 * u, 32 * u + 32)
-            nc.vector.tensor_tensor(z_out[:, c], parts[u][:].rearrange("p t (c i) -> p c t i", i=4), last_in[:, c], ADD)
+            z_out = zg[u][:].rearrange("p (c i) t -> p c t i", i=4)
+            z_in = parts[u][:].rearrange("p t (c i) -> p c t i", i=4)
+            last_in = terms[2][:, :, 128 * u : 128 * u + 128].rearrange("p t (c i) -> p c t i", i=4)
+            nc.vector.tensor_tensor(z_out, z_in, last_in, ADD)
         for u in range(2):
-            quantize(z_codes, z_scales, zg_flat, 128 * u, 128 * u + 128)
+            quantize(z_codes[u], z_scales[u], zg[u][:].rearrange("p v j -> p (v j)"), 0, 128)
 
         staged = [keep.tile([P, 2, 128], F32, name=f"staged{b}") for b in range(4)]
         out_view = out.rearrange("(m p) v -> p m v", p=P)
@@ -177,14 +166,14 @@ def tile_picked_sage_silu_e_kernel(tc, xT, w1, w2, gate, offs, pos1, pos2, pos3,
                         out=o_bank[:, i, :],
                         lhsT=w2_codes[:, 128 * m : 128 * m + 128].bitcast(FP8X4),
                         lhsT_scale=w2_scales[:, 128 * m : 128 * m + 128],
-                        rhs=z_codes[:, 128 * u : 128 * u + 128].bitcast(FP8X4),
-                        rhs_scale=z_scales[:, 128 * u : 128 * u + 128],
+                        rhs=z_codes[u][:].bitcast(FP8X4),
+                        rhs_scale=z_scales[u][:],
                         start=True,
                         stop=True,
                     )
-                if g == 0:
-                    nc.scalar.copy(staged[b][:], o_bank[:])
-                    nc.sync.dma_start(out_view[:, 2 * g : 2 * g + 2, 128 * u : 128 * u + 128], staged[b][:])
-                else:
+                if b == 2:
                     nc.vector.tensor_copy(staged[b][:], o_bank[:])
-                    nc.scalar.dma_start(out_view[:, 2 * g : 2 * g + 2, 128 * u : 128 * u + 128], staged[b][:])
+                else:
+                    nc.scalar.copy(staged[b][:], o_bank[:])
+                queue = nc.scalar if b == 3 else nc.sync
+                queue.dma_start(out_view[:, 2 * g : 2 * g + 2, 128 * u : 128 * u + 128], staged[b][:])

from contextlib import ExitStack

import concourse.mybir as mybir
from concourse.masks import make_identity

FLOPS = 2 * 512 * 512 * 512 + 2 * 512 * 512 * 256

F32 = mybir.dt.float32
BF16 = mybir.dt.bfloat16
U32 = mybir.dt.uint32
U16 = mybir.dt.uint16
U8 = mybir.dt.uint8
FP8X4 = mybir.dt.float8_e4m3fn_x4
MULT = mybir.AluOpType.mult
ADD = mybir.AluOpType.add
SILU = mybir.ActivationFunctionType.Silu

P = 128
K, T, S, V, H, N, D = 512, 2048, 512, 256, 512, 512, 3
PACK = 4


def tile_picked_sage_silu_e_kernel(tc, xT, w1, w2, gate, offs, pos1, pos2, pos3, out):
    nc = tc.nc
    with ExitStack() as ctx:
        keep = ctx.enter_context(tc.tile_pool(name="keep", bufs=1))
        psum = ctx.enter_context(tc.psum_pool(name="psum", bufs=1))

        offs_t = keep.tile([P, S // 16], U16, name="offs_t")
        nc.sync.dma_start(offs_t[:], offs)
        planes = [keep.tile([P, T], F32, name=f"plane{j}") for j in range(PACK)]
        x_view = xT.rearrange("(p j) t -> p j t", j=PACK)
        w1_raw = keep.tile([P, PACK, H], F32, name="w1_raw")
        w2_raw = keep.tile([P, PACK, N], F32, name="w2_raw")
        gates = keep.tile([P, D, V], F32, name="gates")
        pos_t = [keep.tile([P, V // 16], U16, name=f"pos_t{d}") for d in range(D)]

        for j in range(PACK):
            nc.sync.dma_start(planes[j][:], x_view[:, j, :])
        nc.sync.dma_start(w1_raw[:], w1.rearrange("(p j) c -> p j c", j=PACK))
        for d, pos in enumerate((pos1, pos2, pos3)):
            nc.sync.dma_start(gates[:, d, :], gate[d])
            nc.sync.dma_start(pos_t[d][:], pos)
        w2_view = w2.rearrange("(g j r) m -> j g r m", j=PACK, r=8)
        for j in range(PACK):
            nc.sync.dma_start(w2_raw[:, j, :], w2_view[j])

        warm = keep.tile([P, 1], F32, name="warm")
        warm_out = keep.tile([P, 1], F32, name="warm_out")
        nc.vector.memset(warm[:], 0.0)
        nc.scalar.activation(warm_out[:], warm[:], SILU)
        ident = keep.tile([P, P], F32, name="ident")
        make_identity(nc, ident[:])

        xg = keep.tile([P, S, PACK], BF16, align_bytes=64, name="xg")
        x_codes = keep.tile([P, S], U32, align_bytes=64, name="x_codes")
        x_scales = keep.tile([P, S], U8, align_bytes=64, name="x_scales")
        w1g = [keep.tile([P, P, PACK], BF16, align_bytes=64, name=f"w1g{t}") for t in range(4)]
        w1_codes = [keep.tile([P, P], U32, align_bytes=64, name=f"w1_codes{t}") for t in range(4)]
        w1_scales = [keep.tile([P, P], U8, align_bytes=64, name=f"w1_scales{t}") for t in range(4)]
        w2g = keep.tile([P, N, PACK], BF16, align_bytes=64, name="w2g")
        w2_codes = keep.tile([P, N], U32, align_bytes=64, name="w2_codes")
        w2_scales = keep.tile([P, N], U8, align_bytes=64, name="w2_scales")

        def quantize(codes, scales, grouped, a, b):
            nc.vector.quantize_mx(out=codes[:, a:b].bitcast(FP8X4), scales=scales[:, a:b], in_=grouped[:, PACK * a : PACK * b])

        xg_flat = xg[:].rearrange("p s j -> p (s j)")
        w2g_flat = w2g[:].rearrange("p m j -> p (m j)")

        for j in range(3):
            nc.vector.tensor_copy(xg[:, :, j], planes[j][:].indirect(offs_t[:]))
        for u in range(2):
            nc.vector.tensor_copy(xg[:, 256 * u : 256 * u + 256, 3], planes[3][:].indirect(offs_t[:, 16 * u : 16 * u + 16]))
        for u in range(2):
            quantize(x_codes, x_scales, xg_flat, 256 * u, 256 * u + 256)

        w1_in = w1_raw[:].rearrange("p j (g t r) -> t p g r j", t=4, r=8)
        banks = [psum.tile([P, S], F32, name=f"bank{t}") for t in range(4)]
        h = [keep.tile([P, S], F32, name=f"h{t}") for t in range(4)]

        def cast_w1(t, copy):
            grouped = w1g[t][:].rearrange("p (g r) j -> p g r j", r=8)
            copy(grouped, w1_in[t])

        def quantize_w1(t):
            quantize(w1_codes[t], w1_scales[t], w1g[t][:].rearrange("p m j -> p (m j)"), 0, P)

        def layer1(bank, t, cols):
            nc.tensor.matmul_mx(
                out=bank,
                lhsT=w1_codes[t][:].bitcast(FP8X4),
                lhsT_scale=w1_scales[t][:],
                rhs=x_codes[:, cols].bitcast(FP8X4),
                rhs_scale=x_scales[:, cols],
                start=True,
                stop=True,
            )

        cast_w1(0, nc.vector.tensor_copy)
        cast_w1(1, nc.scalar.copy)
        quantize_w1(0)
        cast_w1(2, nc.vector.tensor_copy)
        quantize_w1(1)
        cast_w1(3, nc.vector.tensor_copy)
        quantize_w1(2)
        quantize_w1(3)
        bank0b = psum.tile([P, 256], F32, name="part0")
        for u, bank in enumerate((banks[0][:, 0:256], bank0b[:])):
            cols = slice(256 * u, 256 * u + 256)
            layer1(bank, 0, cols)
            nc.scalar.activation(h[0][:, cols], bank, SILU)
        for t in range(1, 4):
            layer1(banks[t][:], t, slice(0, S))
            nc.scalar.activation(h[t][:], banks[t][:], SILU)

        terms = [keep.tile([P, 4, V], F32, name=f"term{d}") for d in range(D)]
        parts = [psum.tile([P, 4, 128], F32, name=f"part{u}") for u in range(2)]

        def fetch(t, d):
            nc.vector.tensor_tensor(terms[d][:, t, :], h[t][:].indirect(pos_t[d][:]), gates[:, d, :], MULT)

        def add_two(t):
            flipped = psum.tile([P, 2, 128], F32, name=f"flipped{t % 2}")
            for u in range(2):
                for d in range(2):
                    nc.tensor.matmul(flipped[:, u, :], terms[d][:, t, 128 * u : 128 * u + 128], ident[:], is_transpose=True, start=d == 0, stop=d == 1)
            flat = keep.tile([P, 2, 128], F32, name=f"flat{t}")
            nc.scalar.copy(flat[:], flipped[:])
            for u in range(2):
                nc.tensor.transpose(parts[u][:, t, :], flat[:, u, :], ident[:])

        w2_in4 = w2_raw[:].rearrange("p j (c i) -> p c j i", i=4)
        w2_out4 = w2g[:].rearrange("p (c i) j -> p c j i", i=4)

        for t in range(4):
            fetch(t, 0)
            fetch(t, 1)
            add_two(t)
            nc.scalar.copy(w2_out4[:, 32 * t : 32 * t + 32], w2_in4[:, 32 * t : 32 * t + 32])
        for t in range(4):
            fetch(t, 2)
            if t < 2:
                quantize(w2_codes, w2_scales, w2g_flat, 256 * t, 256 * t + 256)

        zg = [keep.tile([P, 128, PACK], BF16, align_bytes=64, name=f"zg{u}") for u in range(2)]
        z_codes = [keep.tile([P, 128], U32, align_bytes=64, name=f"z_codes{u}") for u in range(2)]
        z_scales = [keep.tile([P, 128], U8, align_bytes=64, name=f"z_scales{u}") for u in range(2)]
        for u in range(2):
            z_out = zg[u][:].rearrange("p (c i) t -> p c t i", i=4)
            z_in = parts[u][:].rearrange("p t (c i) -> p c t i", i=4)
            last_in = terms[2][:, :, 128 * u : 128 * u + 128].rearrange("p t (c i) -> p c t i", i=4)
            nc.vector.tensor_tensor(z_out, z_in, last_in, ADD)
        for u in range(2):
            quantize(z_codes[u], z_scales[u], zg[u][:].rearrange("p v j -> p (v j)"), 0, 128)

        staged = [keep.tile([P, 2, 128], F32, name=f"staged{b}") for b in range(4)]
        out_view = out.rearrange("(m p) v -> p m v", p=P)
        for u in range(2):
            for g in range(2):
                b = 2 * u + g
                o_bank = psum.tile([P, 2, 128], F32, name=f"bank{b}")
                for i in range(2):
                    m = 2 * g + i
                    nc.tensor.matmul_mx(
                        out=o_bank[:, i, :],
                        lhsT=w2_codes[:, 128 * m : 128 * m + 128].bitcast(FP8X4),
                        lhsT_scale=w2_scales[:, 128 * m : 128 * m + 128],
                        rhs=z_codes[u][:].bitcast(FP8X4),
                        rhs_scale=z_scales[u][:],
                        start=True,
                        stop=True,
                    )
                if b == 2:
                    nc.vector.tensor_copy(staged[b][:], o_bank[:])
                else:
                    nc.scalar.copy(staged[b][:], o_bank[:])
                queue = nc.scalar if b == 3 else nc.sync
                queue.dma_start(out_view[:, 2 * g : 2 * g + 2, 128 * u : 128 * u + 128], staged[b][:])
